import numpy as np
import ml_dtypes


def mxq(x, axis, fmt="e4m3"):
    dtype, down = {"e4m3": (ml_dtypes.float8_e4m3fn, 7), "e5m2": (ml_dtypes.float8_e5m2, 14)}[fmt]
    v = np.moveaxis(np.asarray(x, np.float32).astype(ml_dtypes.bfloat16).astype(np.float64), axis, -1)
    blocks = v.reshape(v.shape[:-1] + (-1, 32))
    amax = np.abs(blocks).max(-1, keepdims=True)
    byte = np.maximum(np.where(amax > 0, np.frexp(amax)[1] - 1 + 127, 0) - down, 1)
    scale = np.exp2(byte - 127.0)
    codes = (blocks / scale).astype(np.float32).astype(dtype).astype(np.float64)
    return np.moveaxis((codes * scale).reshape(v.shape), -1, axis)


WIDE = False


def mx_kscale(k):
    if not WIDE:
        return np.ones(k)
    levels = np.array([10, -10, 5, -5, 0])
    if k % 512:
        return np.exp2(np.random.permutation(np.resize(levels, k // 32))).repeat(32)
    a = np.empty((k // 512, 16))
    for p in range(k // 512):
        a[p, :8] = np.random.permutation(np.resize(levels, 8))
        for g in range(8):
            far = levels[np.abs(levels - a[p, g]) >= 10]
            a[p, g + 8] = far[np.random.randint(len(far))]
    return np.exp2(a.ravel()).repeat(32)


BF16 = ml_dtypes.bfloat16


def bf(x):
    return np.asarray(x, np.float32).astype(BF16)


def f64(x):
    return np.asarray(x).astype(np.float64)


E2M1 = np.array([0.0, 0.5, 1.0, 1.5, 2.0, 3.0, 4.0, 6.0, -0.0, -0.5, -1.0, -1.5, -2.0, -3.0, -4.0, -6.0])


def pack_weight(w, fmt):
    k, n = w.shape
    w = f64(bf(w)).reshape(k // 32, 32, n)
    amax = np.abs(w).max(1)
    if fmt == "e4m3":
        byte = np.frexp(amax)[1] - 1 + 127 - 7
    else:
        mant, ex = np.frexp(amax / 6.0)
        byte = np.where(mant > 0.5, ex, ex - 1) + 127
    byte = np.clip(np.where(amax > 0, byte, 1), 1, 254)
    scaled = (w * np.exp2(127.0 - byte)[:, None, :]).reshape(k, n).astype(np.float32)
    by_word = np.ascontiguousarray(scaled.reshape(k // 512, 128, 4, n).transpose(0, 1, 3, 2))
    if fmt == "e4m3":
        words = by_word.astype(ml_dtypes.float8_e4m3fn).view(np.uint8)
    else:
        c = by_word.astype(ml_dtypes.float4_e2m1fn).view(np.uint8) & 0xF
        words = c[..., 0::2] | (c[..., 1::2] << 4)
    return np.ascontiguousarray(words), np.ascontiguousarray(byte.astype(np.uint8).reshape(k // 512, 16, n))


def unpack_weight(words, scales, fmt):
    g, p, n, _ = words.shape
    if fmt == "e4m3":
        vals = np.ascontiguousarray(words).view(ml_dtypes.float8_e4m3fn).astype(np.float64)
    else:
        nib = np.empty((g, p, n, 4), np.uint8)
        nib[..., 0::2] = words & 0xF
        nib[..., 1::2] = words >> 4
        vals = E2M1[nib]
    vals = vals * np.repeat(np.exp2(scales.astype(np.float64) - 127.0), 8, axis=1)[..., None]
    return vals.transpose(0, 1, 3, 2).reshape(g * 512, n)
def pack4(w):
    words, scales = pack_weight(w, "e2m1")
    return words.reshape(words.shape[0], 128, -1), scales


def unpack4(words, scales):
    return unpack_weight(words.reshape(words.shape[0], 128, -1, 2), scales, "e2m1")


def planes(Y):
    n, m = Y.shape
    b = f64(bf(Y)).reshape(n // 32, 32, m)
    amax = np.abs(b).max(1)
    byte = np.clip(np.where(amax > 0, np.frexp(amax)[1] - 1 + 127 - 7, 1), 1, 254)
    codes = (b * np.exp2(127.0 - byte)[:, None, :]).reshape(n, m).astype(np.float32).astype(ml_dtypes.float8_e4m3fn).view(np.uint8)
    words = codes.reshape(n // 512, 128, 4, m).transpose(0, 1, 3, 2)
    return np.ascontiguousarray(words), np.ascontiguousarray(byte.astype(np.uint8).reshape(n // 512, 16, m))


N, D, V, E = 512, 1024, 2048, 1024


def scaled_softmax(logits):
    vocab = logits.shape[-1]
    e = np.exp(logits - logits.max(-1, keepdims=True))
    return vocab * (e / e.sum(-1, keepdims=True))


def residual(p, q):
    d = np.maximum(p - q, 0.0)
    return d / d.mean(-1, keepdims=True)


def setup_inputs():
    s, t = mx_kscale(D), mx_kscale(V)
    h_t = bf(np.random.standard_normal((N, D)) * s)
    w_t_words, w_t_scales = pack4(np.random.standard_normal((D, V)) / np.sqrt(D) / s[:, None])
    q1 = bf(np.random.uniform(0.0, 2.0, (N, V)))
    q2 = bf(np.random.uniform(0.0, 2.0, (N, V)))
    g = bf(np.random.standard_normal(V) * t)
    emb_words, emb_scales = pack4(np.random.standard_normal((V, E)) / np.sqrt(V) / t[:, None])
    return {
        "h_t": h_t,
        "w_t_words": w_t_words,
        "w_t_scales": w_t_scales,
        "q1": q1,
        "q2": q2,
        "g": g,
        "emb_words": emb_words,
        "emb_scales": emb_scales,
    }


def core(h_t, w_t_words, w_t_scales, q1, q2, g, emb_words, emb_scales):
    lt = mxq(f64(h_t), 1, "e4m3") @ unpack4(w_t_words, w_t_scales)
    p = scaled_softmax(lt)
    r1 = residual(p, f64(q1))
    r2 = residual(r1, f64(q2))
    c = r2 * f64(g)[None, :]
    return mxq(c, 1, "e4m3") @ unpack4(emb_words, emb_scales)


def reference(h_t, w_t_words, w_t_scales, q1, q2, g, emb_words, emb_scales):
    R_out = core(h_t, w_t_words, w_t_scales, q1, q2, g, emb_words, emb_scales)
    words, scales = planes(R_out)
    return R_out, words, scales

@@ -1,0 +1,445 @@
+from contextlib import ExitStack
+
+import concourse.mybir as mybir
+from concourse.masks import make_identity
+
+F32 = mybir.dt.float32
+BF16 = mybir.dt.bfloat16
+U32 = mybir.dt.uint32
+I32 = mybir.dt.int32
+U8 = mybir.dt.uint8
+FP8X4 = mybir.dt.float8_e4m3fn_x4
+FP4X4 = mybir.dt.float4_e2m1fn_x4
+ALU = mybir.AluOpType
+ACT = mybir.ActivationFunctionType
+AX = mybir.AxisListType
+
+N, D, V, E = 512, 1024, 2048, 1024
+P = 128
+T = 4
+BANK = 512
+FLOPS = 2 * N * D * V + 2 * N * V * E
+
+ORDER = """
+Lh0b Lh0a Lh1 Lw1 Lws Lw0 hT01 Lw23 Lr0 hT00 hc01v Lh2 hT10 hc00v hq01 Lq0 hq00 Lh3 Lq1 hc10v Lr3 L01 Le hq10
+Lg L00 M01 L03 Lq2 M00 L02 M03 L12 Lq3 M02 L13 Lr1 NM0 M12 L10 X00 M13 L11 X01 Lr2 M10 hT20 X03 Les M11 hT30
+X02 hc20v hc30s mE0v NM1 hq20 X10 A00 L21 X11 L20 X12 A01 L22 X13 L23 M21 mE1s R00s RM1 M23 D1gv M22 R01s G13
+M20 hq30 NM2 mR0s G11 X20 B01 U13s X23 B00 L33 X22 G12 X21 S01v mE2s S00s G10 RM2 M33 D2gv A20 U11s G22 mS0s
+U12s RC0 U10s C00 L31 mR1s R20s L30 B10 T00 U22s G23 M31 K00s B11 S10s L32 C01 U23s S11s M30 T01 M32 K01s mR2v
+mS1v NM3 Q00 X30 RC1 B21 Z00 X31 X32 B20 X33 S21s Q01 C11 Z01 mE3s S20s RM3 D3gv A30 G33 mS2s O01s RC2 C10
+R30s G32 C20 U33s T10 U32s C21 T20 K10s T11 O00s mR3v Q10 T21 B31 K20s ST0 Z10 B30 K11s S31s B32 S30s Q20 S32v
+Z20 K21s Q11 mS3v RC3 Z11 C30 C31 O10s T30 Q21 O11s C32 T31 Z21 K31s ST1 K30v Q30 T32 O21v O20s Z30 K32v Q31
+Q32 Z31 Z32 O31v O30s P3v P2s SH30 ST2 SH31 P1v P1s P2v P3s P0v P0s oQ1 oQ0 oQ2 SC0 oQ3 SC1 SS
+""".split()
+
+A_WIDTH = {0: (1024, 1024), 1: (), 2: (1024,), 3: (1024,)}
+B_WIDTH = {0: (1024, 1024), 1: (1024, 1024), 2: (1024, 1024), 3: (1024, 512, 512)}
+C_WIDTH = {0: (1024, 1024), 1: (1024, 1024), 2: (1024, 1024), 3: (1024, 512, 512)}
+HT_BANK = {0: (4, 5), 1: (6,), 2: (0,), 3: (1,)}
+LT_BANK = {0: (0, 1, 2, 3), 1: (4, 5, 6, 7), 2: (0, 1, 2, 3), 3: (4, 5, 6, 7)}
+PA_BANK = LT_BANK
+CT_BANK = {0: (0, 1), 1: (0, 1), 2: (4, 5), 3: (0, 1, 4)}
+O_BANK = {0: (2, 3), 1: (2, 3), 2: (6, 7), 3: (2, 3)}
+PE_CHUNKS = {0: 0, 1: 4, 2: 2, 3: 2}
+
+
+def tile_specinferrecursiveresidualverify_x2_kernel(
+    tc, h_t, w_t_words, w_t_scales, q1, q2, g, emb_words, emb_scales, out_0, out_1, out_2
+):
+    nc = tc.nc
+    with ExitStack() as ctx:
+        keep = ctx.enter_context(tc.tile_pool(name="keep", bufs=1))
+        psum = ctx.enter_context(tc.psum_pool(name="psum", bufs=1))
+
+        def sb(shape, dtype, name):
+            return keep.tile(shape, dtype, name=name, align_bytes=64)
+
+        ident = sb([P, P], F32, "ident")
+        h_sb = sb([P, T, D], BF16, "h_sb")
+        w_sb = sb([P, 2, 2 * V], U8, "w_sb")
+        w_sc = sb([P, 2, V], U8, "w_sc")
+        emb_sb = sb([P, 4, 2 * E], U8, "emb_sb")
+        emb_sc = sb([P, 4, E], U8, "emb_sc")
+        q1_sb = sb([P, T, V], BF16, "q1_sb")
+        q2_sb = sb([P, T, V], BF16, "q2_sb")
+        g_sb = sb([P, V], BF16, "g_sb")
+        h_codes = sb([P, T, 2, P], U32, "h_codes")
+        h_scale = sb([P, T, 2, P], U8, "h_scale")
+        o_sb = sb([P, T, E], F32, "o_sb")
+        ob = sb([P, E, T], BF16, "ob")
+        o_codes = sb([P, E], U32, "o_codes")
+        o_scale = sb([P, E], U8, "o_scale")
+        hg = [sb([P, 2, P, 4], BF16, "hg%d" % t) for t in range(T)]
+        x = [sb([P, V], F32, "x%d" % t) for t in range(T)]
+        c = [sb([P, V], BF16, "c%d" % t) for t in range(T)]
+        cg = [sb([P, 4, P, 4], BF16, "cg%d" % t) for t in range(T)]
+        cc = [sb([P, 4, P], U32, "cc%d" % t) for t in range(T)]
+        cs = [sb([P, 4, P], U8, "cs%d" % t) for t in range(T)]
+        neg_i = sb([P, P], BF16, "neg_i")
+        diag = [sb([P, P], F32, "diag%d" % t) for t in range(T)]
+        vmax = [sb([P, 8], F32, "vmax%d" % t) for t in range(T)]
+        ssum = [sb([P, 64], F32, "ssum%d" % t) for t in range(T)]
+        smean = [sb([P, 8], F32, "smean%d" % t) for t in range(T)]
+        vmean = [sb([P, 8], F32, "vmean%d" % t) for t in range(T)]
+        sjunk = [sb([P, 8], F32, "sjunk%d" % t) for t in range(T)]
+        vjunk = [sb([P, 8], F32, "vjunk%d" % t) for t in range(T)]
+        vrec = [sb([P, 8], F32, "vrec%d" % t) for t in range(T)]
+
+        h_view = h_t.rearrange("(p t) k -> p t k", t=T)
+        q1_view = q1.rearrange("(p t) v -> p t v", t=T)
+        q2_view = q2.rearrange("(p t) v -> p t v", t=T)
+        o_view = out_0.rearrange("(p t) m -> p t m", t=T)
+        w_view = w_t_words.rearrange("g p x -> p g x")
+        ws_view = w_t_scales.rearrange("g q n -> q g n")
+        e_view = emb_words.rearrange("g p x -> p g x")
+        es_view = emb_scales.rearrange("g q n -> q g n")
+        oc_view = out_1[0].rearrange("p m t -> p (m t)")
+
+        steps = {}
+        live = {}
+
+        def bank(i, shape, name):
+            live[name] = psum.tile(shape, F32, name=name, tag="b%d" % i)
+            return live[name]
+
+        def load_h(t, a=0, b=D):
+            nc.sync.dma_start(out=h_sb[:, t, a:b], in_=h_view[:, t, a:b])
+
+        def load_w(a, b):
+            nc.sync.dma_start(
+                out=w_sb[:, :, 2 * a : 2 * b].bitcast(I32), in_=w_view[:, :, 2 * a : 2 * b].bitcast(I32)
+            )
+
+        def load_ws():
+            for q in range(4):
+                nc.sync.dma_start(
+                    out=w_sc[32 * q : 32 * q + 4, :, :].bitcast(I32), in_=ws_view[4 * q : 4 * q + 4, :, :].bitcast(I32)
+                )
+
+        def load_es():
+            for q in range(4):
+                nc.sync.dma_start(
+                    out=emb_sc[32 * q : 32 * q + 4, :, :].bitcast(I32),
+                    in_=es_view[4 * q : 4 * q + 4, :, :].bitcast(I32),
+                )
+
+        def load_q(sbuf, view, t):
+            nc.sync.dma_start(out=sbuf[:, t, :], in_=view[:, t, :])
+
+        def load_g():
+            nc.sync.dma_start(out=g_sb[:], in_=g.partition_broadcast(P))
+
+        def load_e():
+            nc.sync.dma_start(out=emb_sb[:].bitcast(I32), in_=e_view.bitcast(I32))
+
+        steps["Lws"] = load_ws
+        steps["Les"] = load_es
+        steps["Lg"] = load_g
+        steps["Le"] = load_e
+        for t in range(T):
+            steps["Lh%d" % t] = lambda t=t: load_h(t)
+            steps["Lq%d" % t] = lambda t=t: load_q(q1_sb, q1_view, t)
+            steps["Lr%d" % t] = lambda t=t: load_q(q2_sb, q2_view, t)
+        steps["Lh0a"] = lambda: load_h(0, 0, 512)
+        steps["Lh0b"] = lambda: load_h(0, 512, 1024)
+        for j in range(4):
+            steps["Lw%d" % j] = lambda j=j: load_w(512 * j, 512 * (j + 1))
+        steps["Lw23"] = lambda: load_w(1024, 2048)
+
+        def h_turn(t, a, b):
+            hw = h_sb[:, t, :].bitcast(F32)
+            xt = bank(HT_BANK[t][a], [P, b - a, 2, P], "xt%d%d" % (t, a))
+            for gi in range(a, b):
+                for u in range(2):
+                    nc.tensor.transpose(xt[:, gi - a, u, :], hw[:, 256 * gi + u : 256 * (gi + 1) : 2], ident[:])
+
+        def h_copy(t, a, b, eng):
+            out = hg[t][:, a:b].rearrange("p g r j -> p g (r j)").bitcast(F32).rearrange("p g (r u) -> p g r u", u=2)
+            in_ = live["xt%d%d" % (t, a)][:].rearrange("p g u r -> p g r u")
+            if eng == 0:
+                nc.scalar.copy(out=out, in_=in_)
+            else:
+                nc.vector.tensor_copy(out=out, in_=in_)
+
+        def h_quant(t, a, b):
+            nc.vector.quantize_mx(
+                out=h_codes[:, t, a:b].rearrange("p g r -> p (g r)").bitcast(FP8X4),
+                scales=h_scale[:, t, a:b].rearrange("p g r -> p (g r)"),
+                in_=hg[t][:, a:b].rearrange("p g r j -> p (g r j)"),
+            )
+
+        def lt_chunk(t, j):
+            acc = bank(LT_BANK[t][j], [P, BANK], "acc%d%d" % (t, j))
+            for gi in range(2):
+                nc.tensor.matmul_mx(
+                    out=acc[:],
+                    lhsT=h_codes[:, t, gi, :].bitcast(FP8X4),
+                    lhsT_scale=h_scale[:, t, gi, :],
+                    rhs=w_sb[:, gi, 2 * BANK * j : 2 * BANK * (j + 1)].bitcast(FP4X4),
+                    rhs_scale=w_sc[:, gi, BANK * j : BANK * (j + 1)],
+                    start=(gi == 0),
+                    stop=(gi == 1),
+                )
+
+        def row_max(t, j):
+            nc.vector.tensor_reduce(
+                out=vmax[t][:, j : j + 1], in_=live["acc%d%d" % (t, j)][:], axis=AX.X, op=ALU.max
+            )
+
+        def neg_max(t):
+            nc.vector.tensor_reduce(out=vmax[t][:, 4:5], in_=vmax[t][:, 0:4], axis=AX.X, op=ALU.max, negate=True)
+
+        def exp_chunk(t, j):
+            nc.scalar.activation(
+                out=x[t][:, BANK * j : BANK * (j + 1)],
+                in_=live["acc%d%d" % (t, j)][:],
+                func=ACT.Exp,
+                bias=vmax[t][:, 4:5],
+                scale=1.0,
+                accum_out=ssum[t][:, j : j + 1],
+            )
+
+        def mean(t, a, n, step, col, sign, eng):
+            if eng == 0:
+                nc.scalar.activation(
+                    out=sjunk[t][:, 0:n],
+                    in_=ssum[t][:, a : a + step * n : step],
+                    func=ACT.Copy,
+                    scale=sign / V,
+                    accum_out=smean[t][:, col : col + 1],
+                )
+                live["mean%d%d" % (t, col)] = smean[t][:, col : col + 1]
+            else:
+                nc.vector.tensor_scalar(
+                    out=vjunk[t][:, 0:n],
+                    in0=ssum[t][:, a : a + step * n : step],
+                    scalar1=sign / V,
+                    scalar2=None,
+                    op0=ALU.mult,
+                    op1=ALU.add,
+                    accum_out=vmean[t][:, col : col + 1],
+                )
+                live["mean%d%d" % (t, col)] = vmean[t][:, col : col + 1]
+
+        def rec_mean(t):
+            nc.vector.reciprocal(out=vrec[t][:, 1:2], in_=live["mean%d0" % t])
+
+        def make_diag(t, eng):
+            if eng == 0:
+                nc.scalar.activation(out=diag[t][:], in_=ident[:], func=ACT.Copy, scale=vrec[t][:, 1:2])
+            else:
+                nc.vector.tensor_scalar(
+                    out=diag[t][:], in0=ident[:], scalar1=vrec[t][:, 1:2], scalar2=None, op0=ALU.mult
+                )
+
+        def pe_diff(t, j):
+            s = slice(BANK * j, BANK * (j + 1))
+            dif = bank(PA_BANK[t][j], [P, BANK], "dif%d%d" % (t, j))
+            nc.tensor.matmul(dif[:], lhsT=neg_i[:], rhs=q1_sb[:, t, s], start=True, stop=False)
+            nc.tensor.matmul(dif[:], lhsT=diag[t][:], rhs=x[t][:, s], start=False, stop=True)
+
+        def piece(widths, k):
+            a = sum(widths[:k])
+            return slice(a, a + widths[k])
+
+        def diff_norm(t, k):
+            s = piece(A_WIDTH[t], k)
+            nc.vector.scalar_tensor_tensor(
+                out=x[t][:, s], in0=x[t][:, s], scalar=vrec[t][:, 1:2], in1=q1_sb[:, t, s], op0=ALU.mult, op1=ALU.subtract
+            )
+
+        def diff(t, q_sb, col, s):
+            nc.vector.scalar_tensor_tensor(
+                out=x[t][:, s],
+                in0=q_sb[:, t, s],
+                scalar=live["mean%d%d" % (t, col)],
+                in1=x[t][:, s],
+                op0=ALU.mult,
+                op1=ALU.add,
+            )
+
+        def relu(t, src, s, col, eng):
+            if eng == 0:
+                nc.scalar.activation(out=x[t][:, s], in_=src, func=ACT.Relu, accum_out=ssum[t][:, col : col + 1])
+            else:
+                nc.vector.tensor_scalar(
+                    out=x[t][:, s],
+                    in0=src,
+                    scalar1=0.0,
+                    scalar2=None,
+                    op0=ALU.max,
+                    op1=ALU.add,
+                    accum_out=ssum[t][:, col : col + 1],
+                )
+
+        def relu1(t, k, eng):
+            s = piece(A_WIDTH[t], k)
+            relu(t, x[t][:, s], s, 8 + 4 * k, eng)
+
+        def pe_relu(t, j, eng):
+            col = 8 + 4 * (len(A_WIDTH[t]) + j - (4 - PE_CHUNKS[t]))
+            relu(t, live["dif%d%d" % (t, j)][:], slice(BANK * j, BANK * (j + 1)), col, eng)
+
+        def relu2(t, k, eng):
+            s = piece(B_WIDTH[t], k)
+            relu(t, x[t][:, s], s, 24 + 4 * k, eng)
+
+        def recip(t):
+            nc.vector.reciprocal(out=vrec[t][:, 0:1], in_=live["mean%d2" % t])
+
+        def c_part(t, k):
+            a = sum(C_WIDTH[t][:k])
+            s = slice(a, a + C_WIDTH[t][k])
+            nc.vector.scalar_tensor_tensor(
+                out=c[t][:, s], in0=x[t][:, s], scalar=vrec[t][:, 0:1], in1=g_sb[:, s], op0=ALU.mult, op1=ALU.mult
+            )
+
+        def groups(t, k):
+            a = sum(C_WIDTH[t][:k]) // 512
+            return a, a + C_WIDTH[t][k] // 512
+
+        def c_turn(t, k):
+            cw = c[t][:].bitcast(F32)
+            a, b = groups(t, k)
+            ct = bank(CT_BANK[t][k], [P, b - a, 2, P], "ct%d%d" % (t, k))
+            for gi in range(a, b):
+                for u in range(2):
+                    nc.tensor.transpose(ct[:, gi - a, u, :], cw[:, 256 * gi + u : 256 * (gi + 1) : 2], ident[:])
+
+        def c_copy(t, k, eng):
+            a, b = groups(t, k)
+            out = cg[t][:, a:b].rearrange("p g r j -> p g (r j)").bitcast(F32).rearrange("p g (r u) -> p g r u", u=2)
+            in_ = live["ct%d%d" % (t, k)][:].rearrange("p g u r -> p g r u")
+            if eng == 0:
+                nc.scalar.copy(out=out, in_=in_)
+            else:
+                nc.vector.tensor_copy(out=out, in_=in_)
+
+        def c_quant(t, k):
+            a, b = groups(t, k)
+            nc.vector.quantize_mx(
+                out=cc[t][:, a:b].rearrange("p g r -> p (g r)").bitcast(FP8X4),
+                scales=cs[t][:, a:b].rearrange("p g r -> p (g r)"),
+                in_=cg[t][:, a:b].rearrange("p g r j -> p (g r j)"),
+            )
+
+        def second(t, k):
+            a, b = groups(t, k)
+            if a == 0:
+                for eh in range(2):
+                    bank(O_BANK[t][eh], [P, BANK], "o%d%d" % (t, eh))
+            for gi in range(a, b):
+                for eh in range(2):
+                    nc.tensor.matmul_mx(
+                        out=live["o%d%d" % (t, eh)][:],
+                        lhsT=cc[t][:, gi, :].bitcast(FP8X4),
+                        lhsT_scale=cs[t][:, gi, :],
+                        rhs=emb_sb[:, gi, 2 * BANK * eh : 2 * BANK * (eh + 1)].bitcast(FP4X4),
+                        rhs_scale=emb_sc[:, gi, BANK * eh : BANK * (eh + 1)],
+                        start=(gi == 0),
+                        stop=(gi == 3),
+                    )
+
+        def out_copy(t, eh, eng):
+            dst = o_sb[:, t, BANK * eh : BANK * (eh + 1)]
+            src = live["o%d%d" % (t, eh)][:]
+            if eng == 0:
+                nc.scalar.copy(out=dst, in_=src)
+            else:
+                nc.vector.tensor_copy(out=dst, in_=src)
+
+        def store(t):
+            nc.sync.dma_start(out=o_view[:, t, :], in_=o_sb[:, t, :])
+
+        def store_half(t, eh):
+            s = slice(BANK * eh, BANK * (eh + 1))
+            nc.sync.dma_start(out=o_view[:, t, s], in_=o_sb[:, t, s])
+
+        def pack(a, b, eng):
+            out = ob[:, a:b, :]
+            in_ = o_sb[:, :, a:b].rearrange("p t m -> p m t")
+            if eng == 0:
+                nc.scalar.copy(out=out, in_=in_)
+            else:
+                nc.vector.tensor_copy(out=out, in_=in_)
+
+        def out_quant(k):
+            s = slice(256 * k, 256 * (k + 1))
+            nc.vector.quantize_mx(
+                out=o_codes[:, s].bitcast(FP8X4), scales=o_scale[:, s], in_=ob[:, s, :].rearrange("p m t -> p (m t)")
+            )
+
+        def store_codes(eh):
+            s = slice(BANK * eh, BANK * (eh + 1))
+            nc.sync.dma_start(
+                out=oc_view[:, 4 * BANK * eh : 4 * BANK * (eh + 1)].bitcast(I32), in_=o_codes[:, s].bitcast(I32)
+            )
+
+        def store_scales():
+            for q in range(4):
+                nc.scalar.dma_start(
+                    out=out_2[0, 4 * q : 4 * q + 4, :].bitcast(I32), in_=o_scale[32 * q : 32 * q + 4, :].bitcast(I32)
+                )
+
+        for t in range(T):
+            for a, b in ((0, 1), (1, 2)) if t == 0 else ((0, 2),):
+                steps["hT%d%d" % (t, a)] = lambda t=t, a=a, b=b: h_turn(t, a, b)
+                steps["hc%d%ds" % (t, a)] = lambda t=t, a=a, b=b: h_copy(t, a, b, 0)
+                steps["hc%d%dv" % (t, a)] = lambda t=t, a=a, b=b: h_copy(t, a, b, 1)
+                steps["hq%d%d" % (t, a)] = lambda t=t, a=a, b=b: h_quant(t, a, b)
+            steps["NM%d" % t] = lambda t=t: neg_max(t)
+            for eng, z in ((0, "s"), (1, "v")):
+                n1 = len(A_WIDTH[t]) + PE_CHUNKS[t]
+                n2 = len(B_WIDTH[t])
+                pos = 1.0 if PE_CHUNKS[t] else -1.0
+                steps["mE%d" % t + z] = lambda t=t, eng=eng, pos=pos: mean(t, 0, 4, 1, 0, pos, eng)
+                steps["mR%d" % t + z] = lambda t=t, eng=eng, n1=n1: mean(t, 8, n1, 4, 1, -1.0, eng)
+                steps["mS%d" % t + z] = lambda t=t, eng=eng, n2=n2: mean(t, 24, n2, 4, 2, 1.0, eng)
+                steps["D%dg" % t + z] = lambda t=t, eng=eng: make_diag(t, eng)
+            steps["RC%d" % t] = lambda t=t: recip(t)
+            steps["ST%d" % t] = lambda t=t: store(t)
+            steps["RM%d" % t] = lambda t=t: rec_mean(t)
+            for j in range(4):
+                steps["G%d%d" % (t, j)] = lambda t=t, j=j: pe_diff(t, j)
+                steps["U%d%ds" % (t, j)] = lambda t=t, j=j: pe_relu(t, j, 0)
+                steps["U%d%dv" % (t, j)] = lambda t=t, j=j: pe_relu(t, j, 1)
+                steps["L%d%d" % (t, j)] = lambda t=t, j=j: lt_chunk(t, j)
+                steps["M%d%d" % (t, j)] = lambda t=t, j=j: row_max(t, j)
+                steps["X%d%d" % (t, j)] = lambda t=t, j=j: exp_chunk(t, j)
+            for k in range(len(A_WIDTH[t])):
+                if PE_CHUNKS[t]:
+                    steps["A%d%d" % (t, k)] = lambda t=t, k=k: diff_norm(t, k)
+                else:
+                    steps["A%d%d" % (t, k)] = lambda t=t, k=k: diff(t, q1_sb, 0, piece(A_WIDTH[t], k))
+                for eng, z in ((0, "s"), (1, "v")):
+                    steps["R%d%d" % (t, k) + z] = lambda t=t, k=k, eng=eng: relu1(t, k, eng)
+            for k in range(len(B_WIDTH[t])):
+                steps["B%d%d" % (t, k)] = lambda t=t, k=k: diff(t, q2_sb, 1, piece(B_WIDTH[t], k))
+                for eng, z in ((0, "s"), (1, "v")):
+                    steps["S%d%d" % (t, k) + z] = lambda t=t, k=k, eng=eng: relu2(t, k, eng)
+            for hf in range(2):
+                steps["O%d%ds" % (t, hf)] = lambda t=t, hf=hf: out_copy(t, hf, 0)
+                steps["O%d%dv" % (t, hf)] = lambda t=t, hf=hf: out_copy(t, hf, 1)
+                steps["SH%d%d" % (t, hf)] = lambda t=t, hf=hf: store_half(t, hf)
+            for k in range(len(C_WIDTH[t])):
+                steps["C%d%d" % (t, k)] = lambda t=t, k=k: c_part(t, k)
+                steps["T%d%d" % (t, k)] = lambda t=t, k=k: c_turn(t, k)
+                steps["K%d%ds" % (t, k)] = lambda t=t, k=k: c_copy(t, k, 0)
+                steps["K%d%dv" % (t, k)] = lambda t=t, k=k: c_copy(t, k, 1)
+                steps["Q%d%d" % (t, k)] = lambda t=t, k=k: c_quant(t, k)
+                steps["Z%d%d" % (t, k)] = lambda t=t, k=k: second(t, k)
+        for eh in range(2):
+            steps["SC%d" % eh] = lambda eh=eh: store_codes(eh)
+        for k in range(4):
+            steps["P%dv" % k] = lambda k=k: pack(256 * k, 256 * k + 168, 1)
+            steps["P%ds" % k] = lambda k=k: pack(256 * k + 168, 256 * (k + 1), 0)
+            steps["oQ%d" % k] = lambda k=k: out_quant(k)
+        steps["SS"] = store_scales
+
+        with tc.manual_schedule():
+            make_identity(nc, ident[:])
+            nc.vector.memset(w_sc[:].rearrange("p g n -> p (g n)").bitcast(I32), 0)
+            nc.vector.tensor_scalar(out=neg_i[:], in0=ident[:], scalar1=-1.0, scalar2=None, op0=ALU.mult)
+            nc.gpsimd.memset(emb_sc[:].rearrange("p g n -> p (g n)").bitcast(I32), 0)
+            for s in ORDER:
+                steps[s]()

@@ -21,26 +21,29 @@ BANK = 512
 FLOPS = 2 * N * D * V + 2 * N * V * E
 
 ORDER = """
-Lh0b Lh0a Lh1 Lw1 Lws Lw0 hT01 Lw23 Lr0 hT00 hc01v Lh2 hT10 hc00v hq01 Lq0 hq00 Lh3 Lq1 hc10v Lr3 L01 Le hq10
-Lg L00 M01 L03 Lq2 M00 L02 M03 L12 Lq3 M02 L13 Lr1 NM0 M12 L10 X00 M13 L11 X01 Lr2 M10 hT20 X03 Les M11 hT30
-X02 hc20v hc30s mE0v NM1 hq20 X10 A00 L21 X11 L20 X12 A01 L22 X13 L23 M21 mE1s R00s RM1 M23 D1gv M22 R01s G13
-M20 hq30 NM2 mR0s G11 X20 B01 U13s X23 B00 L33 X22 G12 X21 S01v mE2s S00s G10 RM2 M33 D2gv A20 U11s G22 mS0s
-U12s RC0 U10s C00 L31 mR1s R20s L30 B10 T00 U22s G23 M31 K00s B11 S10s L32 C01 U23s S11s M30 T01 M32 K01s mR2v
-mS1v NM3 Q00 X30 RC1 B21 Z00 X31 X32 B20 X33 S21s Q01 C11 Z01 mE3s S20s RM3 D3gv A30 G33 mS2s O01s RC2 C10
-R30s G32 C20 U33s T10 U32s C21 T20 K10s T11 O00s mR3v Q10 T21 B31 K20s ST0 Z10 B30 K11s S31s B32 S30s Q20 S32v
-Z20 K21s Q11 mS3v RC3 Z11 C30 C31 O10s T30 Q21 O11s C32 T31 Z21 K31s ST1 K30v Q30 T32 O21v O20s Z30 K32v Q31
-Q32 Z31 Z32 O31v O30s P3v P2s SH30 ST2 SH31 P1v P1s P2v P3s P0v P0s oQ1 oQ0 oQ2 SC0 oQ3 SC1 SS
+Lh0b mB Lh0a Lh1 mC mW Lws1 mA W Lw1 Lw23 hT01 Lws0 hT00 hc01s hT10 hc00s hq01 Lw0 hq00 hc10v Lh3 Lq0 hq10 L01
+Lh2 L11 M01 L03 Lq1 Les M11 X01 L12 M03 L02 M12 Lr1 X03 L00 M02 Lr0 L13 M00 X02 L10 nI M13 Lq2 X00 hT30 NM0
+M10 Le F0 hT20 hc30s nE0 RM0 NM1 hc20s Lq3 AF0 hq30 A00 Lr3 X12 hq20 Lg X13 A03 L22 Lr2 X11 A02 L21 X10 A01
+L20 M21 mE1s R01s L23 RM1 M22 L31 A10 D1gs L30 R00s G12 M20 R10s M23 M31 G13 U12s NM2 mR0v M30 X20 B00 X23 L32
+U13s B01 X21 L33 X22 M32 S01s mR1v M33 mE2v B10 S00s NM3 RM2 B11 D2gs mS0s X30 G23 RC0 X32 A20 X33 G22 C00 X31
+S11s mE3v C01 T00 S10s RM3 K00v U22s D3gv A30 G33 mS1s R20s RC1 Q00 C10 U23s T01 U33s G32 C11 mR2s R30s B21
+K01s T10 U32s Z00 B20 S21s mR3v Q01 B32 S20s Z01 B30 K10s T11 O00v mS2s O01s RC2 Q10 K11s C20 ST0 Z10 S32s
+S30s B31 T20 Q11 C21 S31s Z11 K20s mS3v RC3 T21 Q20 C30 Z20 C32 K21s C33 O11s T32 C31 T30 T33 Q21 K30s T31
+O10v K33s Z21 K32s Q30 K31v ST1 Q32 Q33 Q31 Z30 O21v O20s Z31 Z32 Z33 O30v O31s SH30 PK0v PK3s SH31 ST2 PK2v
+PK5s PK4v PK1v PK7s PK6v oQ0 oQ1 oQ2 SC0 oQ3 SS SC1
 """.split()
 
-A_WIDTH = {0: (1024, 1024), 1: (), 2: (1024,), 3: (1024,)}
+ONLINE = (0,)
+A_WIDTH = {0: (512, 512, 512, 512), 1: (1024,), 2: (1024,), 3: (1024,)}
+R_WIDTH = {0: (1024, 1024), 1: (1024,), 2: (1024,), 3: (1024,)}
 B_WIDTH = {0: (1024, 1024), 1: (1024, 1024), 2: (1024, 1024), 3: (1024, 512, 512)}
-C_WIDTH = {0: (1024, 1024), 1: (1024, 1024), 2: (1024, 1024), 3: (1024, 512, 512)}
+C_WIDTH = {0: (1024, 1024), 1: (1024, 1024), 2: (1024, 1024), 3: (512, 512, 512, 512)}
 HT_BANK = {0: (4, 5), 1: (6,), 2: (0,), 3: (1,)}
 LT_BANK = {0: (0, 1, 2, 3), 1: (4, 5, 6, 7), 2: (0, 1, 2, 3), 3: (4, 5, 6, 7)}
 PA_BANK = LT_BANK
-CT_BANK = {0: (0, 1), 1: (0, 1), 2: (4, 5), 3: (0, 1, 4)}
+CT_BANK = {0: (0, 1), 1: (0, 1), 2: (4, 5), 3: (0, 1, 4, 5)}
 O_BANK = {0: (2, 3), 1: (2, 3), 2: (6, 7), 3: (2, 3)}
-PE_CHUNKS = {0: 0, 1: 4, 2: 2, 3: 2}
+PE_CHUNKS = {0: 0, 1: 2, 2: 2, 3: 2}
 
 
 def tile_specinferrecursiveresidualverify_x2_kernel(
@@ -75,10 +78,13 @@ def tile_specinferrecursiveresidualverify_x2_kernel(
         cg = [sb([P, 4, P, 4], BF16, "cg%d" % t) for t in range(T)]
         cc = [sb([P, 4, P], U32, "cc%d" % t) for t in range(T)]
         cs = [sb([P, 4, P], U8, "cs%d" % t) for t in range(T)]
+        warm_sb = sb([P, BANK], BF16, "warm_sb")
         neg_i = sb([P, P], BF16, "neg_i")
         diag = [sb([P, P], F32, "diag%d" % t) for t in range(T)]
         vmax = [sb([P, 8], F32, "vmax%d" % t) for t in range(T)]
         ssum = [sb([P, 64], F32, "ssum%d" % t) for t in range(T)]
+        fac = [sb([P, 8], F32, "fac%d" % t) for t in range(T)]
+        afac = [sb([P, 8], F32, "afac%d" % t) for t in range(T)]
         smean = [sb([P, 8], F32, "smean%d" % t) for t in range(T)]
         vmean = [sb([P, 8], F32, "vmean%d" % t) for t in range(T)]
         sjunk = [sb([P, 8], F32, "sjunk%d" % t) for t in range(T)]
@@ -110,11 +116,15 @@ def tile_specinferrecursiveresidualverify_x2_kernel(
                 out=w_sb[:, :, 2 * a : 2 * b].bitcast(I32), in_=w_view[:, :, 2 * a : 2 * b].bitcast(I32)
             )
 
-        def load_ws():
+        def load_ws(a, b):
             for q in range(4):
                 nc.sync.dma_start(
-                    out=w_sc[32 * q : 32 * q + 4, :, :].bitcast(I32), in_=ws_view[4 * q : 4 * q + 4, :, :].bitcast(I32)
+                    out=w_sc[32 * q : 32 * q + 4, :, a:b].bitcast(I32),
+                    in_=ws_view[4 * q : 4 * q + 4, :, a:b].bitcast(I32),
                 )
+
+        def clear_ws(a, b):
+            nc.vector.memset(w_sc[:, :, a:b].bitcast(I32), 0)
 
         def load_es():
             for q in range(4):
@@ -132,7 +142,15 @@ def tile_specinferrecursiveresidualverify_x2_kernel(
         def load_e():
             nc.sync.dma_start(out=emb_sb[:].bitcast(I32), in_=e_view.bitcast(I32))
 
-        steps["Lws"] = load_ws
+        steps["Lws0"] = lambda: load_ws(0, 512)
+        steps["Lws1"] = lambda: load_ws(512, 2048)
+        steps["mA"] = lambda: clear_ws(0, 512)
+        steps["mB"] = lambda: clear_ws(512, 2048)
+        steps["mC"] = lambda: nc.gpsimd.memset(emb_sc[:].rearrange("p g n -> p (g n)").bitcast(I32), 0)
+        steps["nI"] = lambda: nc.vector.tensor_scalar(
+            out=neg_i[:], in0=ident[:], scalar1=-1.0, scalar2=None, op0=ALU.mult
+        )
+        steps["mW"] = lambda: nc.vector.memset(warm_sb[:], 0.0)
         steps["Les"] = load_es
         steps["Lg"] = load_g
         steps["Le"] = load_e
@@ -183,18 +201,47 @@ def tile_specinferrecursiveresidualverify_x2_kernel(
 
         def row_max(t, j):
             nc.vector.tensor_reduce(
-                out=vmax[t][:, j : j + 1], in_=live["acc%d%d" % (t, j)][:], axis=AX.X, op=ALU.max
+                out=vmax[t][:, j : j + 1],
+                in_=live["acc%d%d" % (t, j)][:],
+                axis=AX.X,
+                op=ALU.max,
+                negate=t in ONLINE,
             )
 
         def neg_max(t):
-            nc.vector.tensor_reduce(out=vmax[t][:, 4:5], in_=vmax[t][:, 0:4], axis=AX.X, op=ALU.max, negate=True)
+            if t in ONLINE:
+                nc.vector.tensor_reduce(out=vmax[t][:, 4:5], in_=vmax[t][:, 0:4], axis=AX.X, op=ALU.min)
+            else:
+                nc.vector.tensor_reduce(out=vmax[t][:, 4:5], in_=vmax[t][:, 0:4], axis=AX.X, op=ALU.max, negate=True)
+
+        def factors(t):
+            nc.scalar.activation(
+                out=fac[t][:, 0:4], in_=vmax[t][:, 0:4], func=ACT.Exp, bias=vmax[t][:, 4:5], scale=-1.0
+            )
+
+        def online_mean(t):
+            nc.vector.scalar_tensor_tensor(
+                out=vjunk[t][:, 0:4],
+                in0=fac[t][:, 0:4],
+                scalar=1.0 / V,
+                in1=ssum[t][:, 0:4],
+                op0=ALU.mult,
+                op1=ALU.mult,
+                accum_out=vmean[t][:, 0:1],
+            )
+            live["mean%d0" % t] = vmean[t][:, 0:1]
+
+        def online_scale(t):
+            nc.vector.tensor_scalar(
+                out=afac[t][:, 0:4], in0=fac[t][:, 0:4], scalar1=vrec[t][:, 1:2], scalar2=None, op0=ALU.mult
+            )
 
         def exp_chunk(t, j):
             nc.scalar.activation(
                 out=x[t][:, BANK * j : BANK * (j + 1)],
                 in_=live["acc%d%d" % (t, j)][:],
                 func=ACT.Exp,
-                bias=vmax[t][:, 4:5],
+                bias=vmax[t][:, j : j + 1] if t in ONLINE else vmax[t][:, 4:5],
                 scale=1.0,
                 accum_out=ssum[t][:, j : j + 1],
             )
@@ -245,7 +292,12 @@ def tile_specinferrecursiveresidualverify_x2_kernel(
         def diff_norm(t, k):
             s = piece(A_WIDTH[t], k)
             nc.vector.scalar_tensor_tensor(
-                out=x[t][:, s], in0=x[t][:, s], scalar=vrec[t][:, 1:2], in1=q1_sb[:, t, s], op0=ALU.mult, op1=ALU.subtract
+                out=x[t][:, s],
+                in0=x[t][:, s],
+                scalar=afac[t][:, k : k + 1] if t in ONLINE else vrec[t][:, 1:2],
+                in1=q1_sb[:, t, s],
+                op0=ALU.mult,
+                op1=ALU.subtract,
             )
 
         def diff(t, q_sb, col, s):
@@ -273,11 +325,11 @@ def tile_specinferrecursiveresidualverify_x2_kernel(
                 )
 
         def relu1(t, k, eng):
-            s = piece(A_WIDTH[t], k)
+            s = piece(R_WIDTH[t], k)
             relu(t, x[t][:, s], s, 8 + 4 * k, eng)
 
         def pe_relu(t, j, eng):
-            col = 8 + 4 * (len(A_WIDTH[t]) + j - (4 - PE_CHUNKS[t]))
+            col = 8 + 4 * (len(R_WIDTH[t]) + j - (4 - PE_CHUNKS[t]))
             relu(t, live["dif%d%d" % (t, j)][:], slice(BANK * j, BANK * (j + 1)), col, eng)
 
         def relu2(t, k, eng):
@@ -355,9 +407,10 @@ def tile_specinferrecursiveresidualverify_x2_kernel(
             s = slice(BANK * eh, BANK * (eh + 1))
             nc.sync.dma_start(out=o_view[:, t, s], in_=o_sb[:, t, s])
 
-        def pack(a, b, eng):
-            out = ob[:, a:b, :]
-            in_ = o_sb[:, :, a:b].rearrange("p t m -> p m t")
+        def pack(k, eng):
+            s = slice(128 * k, 128 * (k + 1))
+            out = ob[:, s, :]
+            in_ = o_sb[:, :, s].rearrange("p t m -> p m t")
             if eng == 0:
                 nc.scalar.copy(out=out, in_=in_)
             else:
@@ -389,7 +442,7 @@ def tile_specinferrecursiveresidualverify_x2_kernel(
                 steps["hq%d%d" % (t, a)] = lambda t=t, a=a, b=b: h_quant(t, a, b)
             steps["NM%d" % t] = lambda t=t: neg_max(t)
             for eng, z in ((0, "s"), (1, "v")):
-                n1 = len(A_WIDTH[t]) + PE_CHUNKS[t]
+                n1 = len(R_WIDTH[t]) + PE_CHUNKS[t]
                 n2 = len(B_WIDTH[t])
                 pos = 1.0 if PE_CHUNKS[t] else -1.0
                 steps["mE%d" % t + z] = lambda t=t, eng=eng, pos=pos: mean(t, 0, 4, 1, 0, pos, eng)
@@ -398,6 +451,9 @@ def tile_specinferrecursiveresidualverify_x2_kernel(
                 steps["D%dg" % t + z] = lambda t=t, eng=eng: make_diag(t, eng)
             steps["RC%d" % t] = lambda t=t: recip(t)
             steps["ST%d" % t] = lambda t=t: store(t)
+            steps["F%d" % t] = lambda t=t: factors(t)
+            steps["nE%d" % t] = lambda t=t: online_mean(t)
+            steps["AF%d" % t] = lambda t=t: online_scale(t)
             steps["RM%d" % t] = lambda t=t: rec_mean(t)
             for j in range(4):
                 steps["G%d%d" % (t, j)] = lambda t=t, j=j: pe_diff(t, j)
@@ -407,10 +463,11 @@ def tile_specinferrecursiveresidualverify_x2_kernel(
                 steps["M%d%d" % (t, j)] = lambda t=t, j=j: row_max(t, j)
                 steps["X%d%d" % (t, j)] = lambda t=t, j=j: exp_chunk(t, j)
             for k in range(len(A_WIDTH[t])):
-                if PE_CHUNKS[t]:
+                if PE_CHUNKS[t] or t in ONLINE:
                     steps["A%d%d" % (t, k)] = lambda t=t, k=k: diff_norm(t, k)
                 else:
                     steps["A%d%d" % (t, k)] = lambda t=t, k=k: diff(t, q1_sb, 0, piece(A_WIDTH[t], k))
+            for k in range(len(R_WIDTH[t])):
                 for eng, z in ((0, "s"), (1, "v")):
                     steps["R%d%d" % (t, k) + z] = lambda t=t, k=k, eng=eng: relu1(t, k, eng)
             for k in range(len(B_WIDTH[t])):
@@ -431,15 +488,20 @@ def tile_specinferrecursiveresidualverify_x2_kernel(
         for eh in range(2):
             steps["SC%d" % eh] = lambda eh=eh: store_codes(eh)
         for k in range(4):
-            steps["P%dv" % k] = lambda k=k: pack(256 * k, 256 * k + 168, 1)
-            steps["P%ds" % k] = lambda k=k: pack(256 * k + 168, 256 * (k + 1), 0)
             steps["oQ%d" % k] = lambda k=k: out_quant(k)
+        for k in range(8):
+            steps["PK%ds" % k] = lambda k=k: pack(k, 0)
+            steps["PK%dv" % k] = lambda k=k: pack(k, 1)
         steps["SS"] = store_scales
+
+        def warm():
+            wb = bank(7, [P, BANK], "warm")
+            for i in range(4):
+                nc.tensor.matmul(wb[:], lhsT=warm_sb[:, 0:P], rhs=warm_sb[:], start=True, stop=True)
+
+        steps["W"] = warm
 
         with tc.manual_schedule():
             make_identity(nc, ident[:])
-            nc.vector.memset(w_sc[:].rearrange("p g n -> p (g n)").bitcast(I32), 0)
-            nc.vector.tensor_scalar(out=neg_i[:], in0=ident[:], scalar1=-1.0, scalar2=None, op0=ALU.mult)
-            nc.gpsimd.memset(emb_sc[:].rearrange("p g n -> p (g n)").bitcast(I32), 0)
             for s in ORDER:
                 steps[s]()

from contextlib import ExitStack

import concourse.mybir as mybir
from concourse.masks import make_identity

F32 = mybir.dt.float32
BF16 = mybir.dt.bfloat16
U32 = mybir.dt.uint32
I32 = mybir.dt.int32
U8 = mybir.dt.uint8
FP8X4 = mybir.dt.float8_e4m3fn_x4
FP4X4 = mybir.dt.float4_e2m1fn_x4
ALU = mybir.AluOpType
ACT = mybir.ActivationFunctionType
AX = mybir.AxisListType

N, D, V, E = 512, 1024, 2048, 1024
P = 128
T = 4
BANK = 512
FLOPS = 2 * N * D * V + 2 * N * V * E

ORDER = """
Lh0b mB Lh0a Lh1 mC mW Lws1 mA W Lw1 Lw23 hT01 Lws0 hT00 hc01s hT10 hc00s hq01 Lw0 hq00 hc10v Lh3 Lq0 hq10 L01
Lh2 L11 M01 L03 Lq1 Les M11 X01 L12 M03 L02 M12 Lr1 X03 L00 M02 Lr0 L13 M00 X02 L10 nI M13 Lq2 X00 hT30 NM0
M10 Le F0 hT20 hc30s nE0 RM0 NM1 hc20s Lq3 AF0 hq30 A00 Lr3 X12 hq20 Lg X13 A03 L22 Lr2 X11 A02 L21 X10 A01
L20 M21 mE1s R01s L23 RM1 M22 L31 A10 D1gs L30 R00s G12 M20 R10s M23 M31 G13 U12s NM2 mR0v M30 X20 B00 X23 L32
U13s B01 X21 L33 X22 M32 S01s mR1v M33 mE2v B10 S00s NM3 RM2 B11 D2gs mS0s X30 G23 RC0 X32 A20 X33 G22 C00 X31
S11s mE3v C01 T00 S10s RM3 K00v U22s D3gv A30 G33 mS1s R20s RC1 Q00 C10 U23s T01 U33s G32 C11 mR2s R30s B21
K01s T10 U32s Z00 B20 S21s mR3v Q01 B32 S20s Z01 B30 K10s T11 O00v mS2s O01s RC2 Q10 K11s C20 ST0 Z10 S32s
S30s B31 T20 Q11 C21 S31s Z11 K20s mS3v RC3 T21 Q20 C30 Z20 C32 K21s C33 O11s T32 C31 T30 T33 Q21 K30s T31
O10v K33s Z21 K32s Q30 K31v ST1 Q32 Q33 Q31 Z30 O21v O20s Z31 Z32 Z33 O30v O31s SH30 PK0v PK3s SH31 ST2 PK2v
PK5s PK4v PK1v PK7s PK6v oQ0 oQ1 oQ2 SC0 oQ3 SS SC1
""".split()

ONLINE = (0,)
A_WIDTH = {0: (512, 512, 512, 512), 1: (1024,), 2: (1024,), 3: (1024,)}
R_WIDTH = {0: (1024, 1024), 1: (1024,), 2: (1024,), 3: (1024,)}
B_WIDTH = {0: (1024, 1024), 1: (1024, 1024), 2: (1024, 1024), 3: (1024, 512, 512)}
C_WIDTH = {0: (1024, 1024), 1: (1024, 1024), 2: (1024, 1024), 3: (512, 512, 512, 512)}
HT_BANK = {0: (4, 5), 1: (6,), 2: (0,), 3: (1,)}
LT_BANK = {0: (0, 1, 2, 3), 1: (4, 5, 6, 7), 2: (0, 1, 2, 3), 3: (4, 5, 6, 7)}
PA_BANK = LT_BANK
CT_BANK = {0: (0, 1), 1: (0, 1), 2: (4, 5), 3: (0, 1, 4, 5)}
O_BANK = {0: (2, 3), 1: (2, 3), 2: (6, 7), 3: (2, 3)}
PE_CHUNKS = {0: 0, 1: 2, 2: 2, 3: 2}


def tile_specinferrecursiveresidualverify_x2_kernel(
    tc, h_t, w_t_words, w_t_scales, q1, q2, g, emb_words, emb_scales, out_0, out_1, out_2
):
    nc = tc.nc
    with ExitStack() as ctx:
        keep = ctx.enter_context(tc.tile_pool(name="keep", bufs=1))
        psum = ctx.enter_context(tc.psum_pool(name="psum", bufs=1))

        def sb(shape, dtype, name):
            return keep.tile(shape, dtype, name=name, align_bytes=64)

        ident = sb([P, P], F32, "ident")
        h_sb = sb([P, T, D], BF16, "h_sb")
        w_sb = sb([P, 2, 2 * V], U8, "w_sb")
        w_sc = sb([P, 2, V], U8, "w_sc")
        emb_sb = sb([P, 4, 2 * E], U8, "emb_sb")
        emb_sc = sb([P, 4, E], U8, "emb_sc")
        q1_sb = sb([P, T, V], BF16, "q1_sb")
        q2_sb = sb([P, T, V], BF16, "q2_sb")
        g_sb = sb([P, V], BF16, "g_sb")
        h_codes = sb([P, T, 2, P], U32, "h_codes")
        h_scale = sb([P, T, 2, P], U8, "h_scale")
        o_sb = sb([P, T, E], F32, "o_sb")
        ob = sb([P, E, T], BF16, "ob")
        o_codes = sb([P, E], U32, "o_codes")
        o_scale = sb([P, E], U8, "o_scale")
        hg = [sb([P, 2, P, 4], BF16, "hg%d" % t) for t in range(T)]
        x = [sb([P, V], F32, "x%d" % t) for t in range(T)]
        c = [sb([P, V], BF16, "c%d" % t) for t in range(T)]
        cg = [sb([P, 4, P, 4], BF16, "cg%d" % t) for t in range(T)]
        cc = [sb([P, 4, P], U32, "cc%d" % t) for t in range(T)]
        cs = [sb([P, 4, P], U8, "cs%d" % t) for t in range(T)]
        warm_sb = sb([P, BANK], BF16, "warm_sb")
        neg_i = sb([P, P], BF16, "neg_i")
        diag = [sb([P, P], F32, "diag%d" % t) for t in range(T)]
        vmax = [sb([P, 8], F32, "vmax%d" % t) for t in range(T)]
        ssum = [sb([P, 64], F32, "ssum%d" % t) for t in range(T)]
        fac = [sb([P, 8], F32, "fac%d" % t) for t in range(T)]
        afac = [sb([P, 8], F32, "afac%d" % t) for t in range(T)]
        smean = [sb([P, 8], F32, "smean%d" % t) for t in range(T)]
        vmean = [sb([P, 8], F32, "vmean%d" % t) for t in range(T)]
        sjunk = [sb([P, 8], F32, "sjunk%d" % t) for t in range(T)]
        vjunk = [sb([P, 8], F32, "vjunk%d" % t) for t in range(T)]
        vrec = [sb([P, 8], F32, "vrec%d" % t) for t in range(T)]

        h_view = h_t.rearrange("(p t) k -> p t k", t=T)
        q1_view = q1.rearrange("(p t) v -> p t v", t=T)
        q2_view = q2.rearrange("(p t) v -> p t v", t=T)
        o_view = out_0.rearrange("(p t) m -> p t m", t=T)
        w_view = w_t_words.rearrange("g p x -> p g x")
        ws_view = w_t_scales.rearrange("g q n -> q g n")
        e_view = emb_words.rearrange("g p x -> p g x")
        es_view = emb_scales.rearrange("g q n -> q g n")
        oc_view = out_1[0].rearrange("p m t -> p (m t)")

        steps = {}
        live = {}

        def bank(i, shape, name):
            live[name] = psum.tile(shape, F32, name=name, tag="b%d" % i)
            return live[name]

        def load_h(t, a=0, b=D):
            nc.sync.dma_start(out=h_sb[:, t, a:b], in_=h_view[:, t, a:b])

        def load_w(a, b):
            nc.sync.dma_start(
                out=w_sb[:, :, 2 * a : 2 * b].bitcast(I32), in_=w_view[:, :, 2 * a : 2 * b].bitcast(I32)
            )

        def load_ws(a, b):
            for q in range(4):
                nc.sync.dma_start(
                    out=w_sc[32 * q : 32 * q + 4, :, a:b].bitcast(I32),
                    in_=ws_view[4 * q : 4 * q + 4, :, a:b].bitcast(I32),
                )

        def clear_ws(a, b):
            nc.vector.memset(w_sc[:, :, a:b].bitcast(I32), 0)

        def load_es():
            for q in range(4):
                nc.sync.dma_start(
                    out=emb_sc[32 * q : 32 * q + 4, :, :].bitcast(I32),
                    in_=es_view[4 * q : 4 * q + 4, :, :].bitcast(I32),
                )

        def load_q(sbuf, view, t):
            nc.sync.dma_start(out=sbuf[:, t, :], in_=view[:, t, :])

        def load_g():
            nc.sync.dma_start(out=g_sb[:], in_=g.partition_broadcast(P))

        def load_e():
            nc.sync.dma_start(out=emb_sb[:].bitcast(I32), in_=e_view.bitcast(I32))

        steps["Lws0"] = lambda: load_ws(0, 512)
        steps["Lws1"] = lambda: load_ws(512, 2048)
        steps["mA"] = lambda: clear_ws(0, 512)
        steps["mB"] = lambda: clear_ws(512, 2048)
        steps["mC"] = lambda: nc.gpsimd.memset(emb_sc[:].rearrange("p g n -> p (g n)").bitcast(I32), 0)
        steps["nI"] = lambda: nc.vector.tensor_scalar(
            out=neg_i[:], in0=ident[:], scalar1=-1.0, scalar2=None, op0=ALU.mult
        )
        steps["mW"] = lambda: nc.vector.memset(warm_sb[:], 0.0)
        steps["Les"] = load_es
        steps["Lg"] = load_g
        steps["Le"] = load_e
        for t in range(T):
            steps["Lh%d" % t] = lambda t=t: load_h(t)
            steps["Lq%d" % t] = lambda t=t: load_q(q1_sb, q1_view, t)
            steps["Lr%d" % t] = lambda t=t: load_q(q2_sb, q2_view, t)
        steps["Lh0a"] = lambda: load_h(0, 0, 512)
        steps["Lh0b"] = lambda: load_h(0, 512, 1024)
        for j in range(4):
            steps["Lw%d" % j] = lambda j=j: load_w(512 * j, 512 * (j + 1))
        steps["Lw23"] = lambda: load_w(1024, 2048)

        def h_turn(t, a, b):
            hw = h_sb[:, t, :].bitcast(F32)
            xt = bank(HT_BANK[t][a], [P, b - a, 2, P], "xt%d%d" % (t, a))
            for gi in range(a, b):
                for u in range(2):
                    nc.tensor.transpose(xt[:, gi - a, u, :], hw[:, 256 * gi + u : 256 * (gi + 1) : 2], ident[:])

        def h_copy(t, a, b, eng):
            out = hg[t][:, a:b].rearrange("p g r j -> p g (r j)").bitcast(F32).rearrange("p g (r u) -> p g r u", u=2)
            in_ = live["xt%d%d" % (t, a)][:].rearrange("p g u r -> p g r u")
            if eng == 0:
                nc.scalar.copy(out=out, in_=in_)
            else:
                nc.vector.tensor_copy(out=out, in_=in_)

        def h_quant(t, a, b):
            nc.vector.quantize_mx(
                out=h_codes[:, t, a:b].rearrange("p g r -> p (g r)").bitcast(FP8X4),
                scales=h_scale[:, t, a:b].rearrange("p g r -> p (g r)"),
                in_=hg[t][:, a:b].rearrange("p g r j -> p (g r j)"),
            )

        def lt_chunk(t, j):
            acc = bank(LT_BANK[t][j], [P, BANK], "acc%d%d" % (t, j))
            for gi in range(2):
                nc.tensor.matmul_mx(
                    out=acc[:],
                    lhsT=h_codes[:, t, gi, :].bitcast(FP8X4),
                    lhsT_scale=h_scale[:, t, gi, :],
                    rhs=w_sb[:, gi, 2 * BANK * j : 2 * BANK * (j + 1)].bitcast(FP4X4),
                    rhs_scale=w_sc[:, gi, BANK * j : BANK * (j + 1)],
                    start=(gi == 0),
                    stop=(gi == 1),
                )

        def row_max(t, j):
            nc.vector.tensor_reduce(
                out=vmax[t][:, j : j + 1],
                in_=live["acc%d%d" % (t, j)][:],
                axis=AX.X,
                op=ALU.max,
                negate=t in ONLINE,
            )

        def neg_max(t):
            if t in ONLINE:
                nc.vector.tensor_reduce(out=vmax[t][:, 4:5], in_=vmax[t][:, 0:4], axis=AX.X, op=ALU.min)
            else:
                nc.vector.tensor_reduce(out=vmax[t][:, 4:5], in_=vmax[t][:, 0:4], axis=AX.X, op=ALU.max, negate=True)

        def factors(t):
            nc.scalar.activation(
                out=fac[t][:, 0:4], in_=vmax[t][:, 0:4], func=ACT.Exp, bias=vmax[t][:, 4:5], scale=-1.0
            )

        def online_mean(t):
            nc.vector.scalar_tensor_tensor(
                out=vjunk[t][:, 0:4],
                in0=fac[t][:, 0:4],
                scalar=1.0 / V,
                in1=ssum[t][:, 0:4],
                op0=ALU.mult,
                op1=ALU.mult,
                accum_out=vmean[t][:, 0:1],
            )
            live["mean%d0" % t] = vmean[t][:, 0:1]

        def online_scale(t):
            nc.vector.tensor_scalar(
                out=afac[t][:, 0:4], in0=fac[t][:, 0:4], scalar1=vrec[t][:, 1:2], scalar2=None, op0=ALU.mult
            )

        def exp_chunk(t, j):
            nc.scalar.activation(
                out=x[t][:, BANK * j : BANK * (j + 1)],
                in_=live["acc%d%d" % (t, j)][:],
                func=ACT.Exp,
                bias=vmax[t][:, j : j + 1] if t in ONLINE else vmax[t][:, 4:5],
                scale=1.0,
                accum_out=ssum[t][:, j : j + 1],
            )

        def mean(t, a, n, step, col, sign, eng):
            if eng == 0:
                nc.scalar.activation(
                    out=sjunk[t][:, 0:n],
                    in_=ssum[t][:, a : a + step * n : step],
                    func=ACT.Copy,
                    scale=sign / V,
                    accum_out=smean[t][:, col : col + 1],
                )
                live["mean%d%d" % (t, col)] = smean[t][:, col : col + 1]
            else:
                nc.vector.tensor_scalar(
                    out=vjunk[t][:, 0:n],
                    in0=ssum[t][:, a : a + step * n : step],
                    scalar1=sign / V,
                    scalar2=None,
                    op0=ALU.mult,
                    op1=ALU.add,
                    accum_out=vmean[t][:, col : col + 1],
                )
                live["mean%d%d" % (t, col)] = vmean[t][:, col : col + 1]

        def rec_mean(t):
            nc.vector.reciprocal(out=vrec[t][:, 1:2], in_=live["mean%d0" % t])

        def make_diag(t, eng):
            if eng == 0:
                nc.scalar.activation(out=diag[t][:], in_=ident[:], func=ACT.Copy, scale=vrec[t][:, 1:2])
            else:
                nc.vector.tensor_scalar(
                    out=diag[t][:], in0=ident[:], scalar1=vrec[t][:, 1:2], scalar2=None, op0=ALU.mult
                )

        def pe_diff(t, j):
            s = slice(BANK * j, BANK * (j + 1))
            dif = bank(PA_BANK[t][j], [P, BANK], "dif%d%d" % (t, j))
            nc.tensor.matmul(dif[:], lhsT=neg_i[:], rhs=q1_sb[:, t, s], start=True, stop=False)
            nc.tensor.matmul(dif[:], lhsT=diag[t][:], rhs=x[t][:, s], start=False, stop=True)

        def piece(widths, k):
            a = sum(widths[:k])
            return slice(a, a + widths[k])

        def diff_norm(t, k):
            s = piece(A_WIDTH[t], k)
            nc.vector.scalar_tensor_tensor(
                out=x[t][:, s],
                in0=x[t][:, s],
                scalar=afac[t][:, k : k + 1] if t in ONLINE else vrec[t][:, 1:2],
                in1=q1_sb[:, t, s],
                op0=ALU.mult,
                op1=ALU.subtract,
            )

        def diff(t, q_sb, col, s):
            nc.vector.scalar_tensor_tensor(
                out=x[t][:, s],
                in0=q_sb[:, t, s],
                scalar=live["mean%d%d" % (t, col)],
                in1=x[t][:, s],
                op0=ALU.mult,
                op1=ALU.add,
            )

        def relu(t, src, s, col, eng):
            if eng == 0:
                nc.scalar.activation(out=x[t][:, s], in_=src, func=ACT.Relu, accum_out=ssum[t][:, col : col + 1])
            else:
                nc.vector.tensor_scalar(
                    out=x[t][:, s],
                    in0=src,
                    scalar1=0.0,
                    scalar2=None,
                    op0=ALU.max,
                    op1=ALU.add,
                    accum_out=ssum[t][:, col : col + 1],
                )

        def relu1(t, k, eng):
            s = piece(R_WIDTH[t], k)
            relu(t, x[t][:, s], s, 8 + 4 * k, eng)

        def pe_relu(t, j, eng):
            col = 8 + 4 * (len(R_WIDTH[t]) + j - (4 - PE_CHUNKS[t]))
            relu(t, live["dif%d%d" % (t, j)][:], slice(BANK * j, BANK * (j + 1)), col, eng)

        def relu2(t, k, eng):
            s = piece(B_WIDTH[t], k)
            relu(t, x[t][:, s], s, 24 + 4 * k, eng)

        def recip(t):
            nc.vector.reciprocal(out=vrec[t][:, 0:1], in_=live["mean%d2" % t])

        def c_part(t, k):
            a = sum(C_WIDTH[t][:k])
            s = slice(a, a + C_WIDTH[t][k])
            nc.vector.scalar_tensor_tensor(
                out=c[t][:, s], in0=x[t][:, s], scalar=vrec[t][:, 0:1], in1=g_sb[:, s], op0=ALU.mult, op1=ALU.mult
            )

        def groups(t, k):
            a = sum(C_WIDTH[t][:k]) // 512
            return a, a + C_WIDTH[t][k] // 512

        def c_turn(t, k):
            cw = c[t][:].bitcast(F32)
            a, b = groups(t, k)
            ct = bank(CT_BANK[t][k], [P, b - a, 2, P], "ct%d%d" % (t, k))
            for gi in range(a, b):
                for u in range(2):
                    nc.tensor.transpose(ct[:, gi - a, u, :], cw[:, 256 * gi + u : 256 * (gi + 1) : 2], ident[:])

        def c_copy(t, k, eng):
            a, b = groups(t, k)
            out = cg[t][:, a:b].rearrange("p g r j -> p g (r j)").bitcast(F32).rearrange("p g (r u) -> p g r u", u=2)
            in_ = live["ct%d%d" % (t, k)][:].rearrange("p g u r -> p g r u")
            if eng == 0:
                nc.scalar.copy(out=out, in_=in_)
            else:
                nc.vector.tensor_copy(out=out, in_=in_)

        def c_quant(t, k):
            a, b = groups(t, k)
            nc.vector.quantize_mx(
                out=cc[t][:, a:b].rearrange("p g r -> p (g r)").bitcast(FP8X4),
                scales=cs[t][:, a:b].rearrange("p g r -> p (g r)"),
                in_=cg[t][:, a:b].rearrange("p g r j -> p (g r j)"),
            )

        def second(t, k):
            a, b = groups(t, k)
            if a == 0:
                for eh in range(2):
                    bank(O_BANK[t][eh], [P, BANK], "o%d%d" % (t, eh))
            for gi in range(a, b):
                for eh in range(2):
                    nc.tensor.matmul_mx(
                        out=live["o%d%d" % (t, eh)][:],
                        lhsT=cc[t][:, gi, :].bitcast(FP8X4),
                        lhsT_scale=cs[t][:, gi, :],
                        rhs=emb_sb[:, gi, 2 * BANK * eh : 2 * BANK * (eh + 1)].bitcast(FP4X4),
                        rhs_scale=emb_sc[:, gi, BANK * eh : BANK * (eh + 1)],
                        start=(gi == 0),
                        stop=(gi == 3),
                    )

        def out_copy(t, eh, eng):
            dst = o_sb[:, t, BANK * eh : BANK * (eh + 1)]
            src = live["o%d%d" % (t, eh)][:]
            if eng == 0:
                nc.scalar.copy(out=dst, in_=src)
            else:
                nc.vector.tensor_copy(out=dst, in_=src)

        def store(t):
            nc.sync.dma_start(out=o_view[:, t, :], in_=o_sb[:, t, :])

        def store_half(t, eh):
            s = slice(BANK * eh, BANK * (eh + 1))
            nc.sync.dma_start(out=o_view[:, t, s], in_=o_sb[:, t, s])

        def pack(k, eng):
            s = slice(128 * k, 128 * (k + 1))
            out = ob[:, s, :]
            in_ = o_sb[:, :, s].rearrange("p t m -> p m t")
            if eng == 0:
                nc.scalar.copy(out=out, in_=in_)
            else:
                nc.vector.tensor_copy(out=out, in_=in_)

        def out_quant(k):
            s = slice(256 * k, 256 * (k + 1))
            nc.vector.quantize_mx(
                out=o_codes[:, s].bitcast(FP8X4), scales=o_scale[:, s], in_=ob[:, s, :].rearrange("p m t -> p (m t)")
            )

        def store_codes(eh):
            s = slice(BANK * eh, BANK * (eh + 1))
            nc.sync.dma_start(
                out=oc_view[:, 4 * BANK * eh : 4 * BANK * (eh + 1)].bitcast(I32), in_=o_codes[:, s].bitcast(I32)
            )

        def store_scales():
            for q in range(4):
                nc.scalar.dma_start(
                    out=out_2[0, 4 * q : 4 * q + 4, :].bitcast(I32), in_=o_scale[32 * q : 32 * q + 4, :].bitcast(I32)
                )

        for t in range(T):
            for a, b in ((0, 1), (1, 2)) if t == 0 else ((0, 2),):
                steps["hT%d%d" % (t, a)] = lambda t=t, a=a, b=b: h_turn(t, a, b)
                steps["hc%d%ds" % (t, a)] = lambda t=t, a=a, b=b: h_copy(t, a, b, 0)
                steps["hc%d%dv" % (t, a)] = lambda t=t, a=a, b=b: h_copy(t, a, b, 1)
                steps["hq%d%d" % (t, a)] = lambda t=t, a=a, b=b: h_quant(t, a, b)
            steps["NM%d" % t] = lambda t=t: neg_max(t)
            for eng, z in ((0, "s"), (1, "v")):
                n1 = len(R_WIDTH[t]) + PE_CHUNKS[t]
                n2 = len(B_WIDTH[t])
                pos = 1.0 if PE_CHUNKS[t] else -1.0
                steps["mE%d" % t + z] = lambda t=t, eng=eng, pos=pos: mean(t, 0, 4, 1, 0, pos, eng)
                steps["mR%d" % t + z] = lambda t=t, eng=eng, n1=n1: mean(t, 8, n1, 4, 1, -1.0, eng)
                steps["mS%d" % t + z] = lambda t=t, eng=eng, n2=n2: mean(t, 24, n2, 4, 2, 1.0, eng)
                steps["D%dg" % t + z] = lambda t=t, eng=eng: make_diag(t, eng)
            steps["RC%d" % t] = lambda t=t: recip(t)
            steps["ST%d" % t] = lambda t=t: store(t)
            steps["F%d" % t] = lambda t=t: factors(t)
            steps["nE%d" % t] = lambda t=t: online_mean(t)
            steps["AF%d" % t] = lambda t=t: online_scale(t)
            steps["RM%d" % t] = lambda t=t: rec_mean(t)
            for j in range(4):
                steps["G%d%d" % (t, j)] = lambda t=t, j=j: pe_diff(t, j)
                steps["U%d%ds" % (t, j)] = lambda t=t, j=j: pe_relu(t, j, 0)
                steps["U%d%dv" % (t, j)] = lambda t=t, j=j: pe_relu(t, j, 1)
                steps["L%d%d" % (t, j)] = lambda t=t, j=j: lt_chunk(t, j)
                steps["M%d%d" % (t, j)] = lambda t=t, j=j: row_max(t, j)
                steps["X%d%d" % (t, j)] = lambda t=t, j=j: exp_chunk(t, j)
            for k in range(len(A_WIDTH[t])):
                if PE_CHUNKS[t] or t in ONLINE:
                    steps["A%d%d" % (t, k)] = lambda t=t, k=k: diff_norm(t, k)
                else:
                    steps["A%d%d" % (t, k)] = lambda t=t, k=k: diff(t, q1_sb, 0, piece(A_WIDTH[t], k))
            for k in range(len(R_WIDTH[t])):
                for eng, z in ((0, "s"), (1, "v")):
                    steps["R%d%d" % (t, k) + z] = lambda t=t, k=k, eng=eng: relu1(t, k, eng)
            for k in range(len(B_WIDTH[t])):
                steps["B%d%d" % (t, k)] = lambda t=t, k=k: diff(t, q2_sb, 1, piece(B_WIDTH[t], k))
                for eng, z in ((0, "s"), (1, "v")):
                    steps["S%d%d" % (t, k) + z] = lambda t=t, k=k, eng=eng: relu2(t, k, eng)
            for hf in range(2):
                steps["O%d%ds" % (t, hf)] = lambda t=t, hf=hf: out_copy(t, hf, 0)
                steps["O%d%dv" % (t, hf)] = lambda t=t, hf=hf: out_copy(t, hf, 1)
                steps["SH%d%d" % (t, hf)] = lambda t=t, hf=hf: store_half(t, hf)
            for k in range(len(C_WIDTH[t])):
                steps["C%d%d" % (t, k)] = lambda t=t, k=k: c_part(t, k)
                steps["T%d%d" % (t, k)] = lambda t=t, k=k: c_turn(t, k)
                steps["K%d%ds" % (t, k)] = lambda t=t, k=k: c_copy(t, k, 0)
                steps["K%d%dv" % (t, k)] = lambda t=t, k=k: c_copy(t, k, 1)
                steps["Q%d%d" % (t, k)] = lambda t=t, k=k: c_quant(t, k)
                steps["Z%d%d" % (t, k)] = lambda t=t, k=k: second(t, k)
        for eh in range(2):
            steps["SC%d" % eh] = lambda eh=eh: store_codes(eh)
        for k in range(4):
            steps["oQ%d" % k] = lambda k=k: out_quant(k)
        for k in range(8):
            steps["PK%ds" % k] = lambda k=k: pack(k, 0)
            steps["PK%dv" % k] = lambda k=k: pack(k, 1)
        steps["SS"] = store_scales

        def warm():
            wb = bank(7, [P, BANK], "warm")
            for i in range(4):
                nc.tensor.matmul(wb[:], lhsT=warm_sb[:, 0:P], rhs=warm_sb[:], start=True, stop=True)

        steps["W"] = warm

        with tc.manual_schedule():
            make_identity(nc, ident[:])
            for s in ORDER:
                steps[s]()
